import numpy as np
import ml_dtypes


def mxq(x, axis, fmt="e4m3"):
    dtype, down = {"e4m3": (ml_dtypes.float8_e4m3fn, 7), "e5m2": (ml_dtypes.float8_e5m2, 14)}[fmt]
    v = np.moveaxis(np.asarray(x, np.float32).astype(ml_dtypes.bfloat16).astype(np.float64), axis, -1)
    blocks = v.reshape(v.shape[:-1] + (-1, 32))
    amax = np.abs(blocks).max(-1, keepdims=True)
    byte = np.maximum(np.where(amax > 0, np.frexp(amax)[1] - 1 + 127, 0) - down, 1)
    scale = np.exp2(byte - 127.0)
    codes = (blocks / scale).astype(np.float32).astype(dtype).astype(np.float64)
    return np.moveaxis((codes * scale).reshape(v.shape), -1, axis)


WIDE = False


def mx_kscale(k):
    if not WIDE:
        return np.ones(k)
    levels = np.array([10, -10, 5, -5, 0])
    if k % 512:
        return np.exp2(np.random.permutation(np.resize(levels, k // 32))).repeat(32)
    a = np.empty((k // 512, 16))
    for p in range(k // 512):
        a[p, :8] = np.random.permutation(np.resize(levels, 8))
        for g in range(8):
            far = levels[np.abs(levels - a[p, g]) >= 10]
            a[p, g + 8] = far[np.random.randint(len(far))]
    return np.exp2(a.ravel()).repeat(32)


def f64(x):
    return np.asarray(x).astype(np.float64)


def striped(idx):
    return np.tile(idx.reshape(-1, 16).T, (8, 1)).astype(np.uint16)


def unstriped(offs):
    return offs[:16].T.reshape(-1).astype(np.int64)


E2M1 = np.array([0.0, 0.5, 1.0, 1.5, 2.0, 3.0, 4.0, 6.0, -0.0, -0.5, -1.0, -1.5, -2.0, -3.0, -4.0, -6.0])


def pack_fp4(w):
    k, n = w.shape
    w = f64(np.asarray(w, np.float32).astype(ml_dtypes.bfloat16)).reshape(k // 32, 32, n)
    amax = np.abs(w).max(1)
    mant, ex = np.frexp(amax / 6.0)
    byte = np.clip(np.where(amax > 0, np.where(mant > 0.5, ex, ex - 1) + 127, 1), 1, 254)
    scaled = (w * np.exp2(127.0 - byte)[:, None, :]).reshape(k, n).astype(np.float32)
    c = np.ascontiguousarray(scaled.reshape(k // 512, 128, 4, n).transpose(0, 1, 3, 2)).astype(ml_dtypes.float4_e2m1fn).view(np.uint8) & 0xF
    words = (c[..., 0::2] | (c[..., 1::2] << 4)).reshape(k // 512, 128, 2 * n)
    return np.ascontiguousarray(words), np.ascontiguousarray(byte.astype(np.uint8).reshape(k // 512, 16, n))


def unpack_fp4(words, scales):
    g, _, n = scales.shape
    words = np.ascontiguousarray(words).reshape(g, 128, n, 2)
    nib = np.empty((g, 128, n, 4), np.uint8)
    nib[..., 0::2] = words & 0xF
    nib[..., 1::2] = words >> 4
    vals = E2M1[nib] * np.repeat(np.exp2(scales.astype(np.float64) - 127.0), 8, axis=1)[..., None]
    return vals.transpose(0, 1, 3, 2).reshape(g * 512, n)


def sigmoid(v):
    return 1.0 / (1.0 + np.exp(-np.maximum(v, -700.0)))


K, T, S, N = 512, 2048, 512, 128


def setup_inputs():
    n = np.random.standard_normal
    s = mx_kscale(K)[:, None]
    packed_w1 = pack_fp4(n((K, N)) / np.sqrt(K) / s)
    packed_w2 = pack_fp4(n((K, N)) / np.sqrt(K) / s)
    return {
        "xT": (n((K, T)) * s).astype(np.float32),
        "res": n((N, T)).astype(np.float32),
        "w1_words": packed_w1[0],
        "w1_scales": packed_w1[1],
        "w2_words": packed_w2[0],
        "w2_scales": packed_w2[1],
        "offs": striped(np.random.permutation(T)[:S]),
    }


def reference(xT, res, w1_words, w1_scales, w2_words, w2_scales, offs):
    r = f64(res)[:, unstriped(offs)]
    xq = mxq(f64(xT)[:, unstriped(offs)], 0, "e4m3")
    g = sigmoid(unpack_fp4(w2_words, w2_scales).T @ xq)
    y = np.tanh(unpack_fp4(w1_words, w1_scales).T @ xq)
    return r + g * (y - r)

@@ -1,0 +1,91 @@
+from contextlib import ExitStack
+
+import concourse.mybir as mybir
+
+K, T, S, N = 512, 2048, 512, 128
+FLOPS = 2 * 2 * K * N * S
+
+F32 = mybir.dt.float32
+BF16 = mybir.dt.bfloat16
+I32 = mybir.dt.int32
+U32 = mybir.dt.uint32
+U16 = mybir.dt.uint16
+U8 = mybir.dt.uint8
+FP8X4 = mybir.dt.float8_e4m3fn_x4
+FP4X4 = mybir.dt.float4_e2m1fn_x4
+ACT = mybir.ActivationFunctionType
+ALU = mybir.AluOpType
+
+P = 128
+PACK = 4
+HALVES = 2
+H = S // HALVES
+LIST_COLS = H // 16
+
+
+def tile_picked_highway_tanh_l_kernel(tc, xT, res, w1_words, w1_scales, w2_words, w2_scales, offs, out):
+    nc = tc.nc
+    with ExitStack() as ctx:
+        keep = ctx.enter_context(tc.tile_pool(name="keep", bufs=1))
+        psum = ctx.enter_context(tc.psum_pool(name="psum", bufs=1))
+
+        offsets = keep.tile([P, S // 16], U16, name="offsets")
+        nc.sync.dma_start(offsets[:], offs)
+
+        x_rows = xT.rearrange("(p t) c -> p t c", t=PACK)
+        planes = []
+        for t in range(PACK):
+            plane = keep.tile([P, T], F32, name=f"plane{t}")
+            nc.sync.dma_start(plane[:], x_rows[:, t, :])
+            planes.append(plane)
+        res_sb = keep.tile([P, T], F32, name="res_sb")
+        nc.sync.dma_start(res_sb[:], res)
+
+        weights = []
+        for name, words, scales, queue in (("w2", w2_words, w2_scales, nc.scalar), ("w1", w1_words, w1_scales, nc.gpsimd)):
+            w_codes = keep.tile([P, 2 * N], U8, name=f"{name}_codes", align_bytes=64)
+            nc.scalar.dma_start(w_codes[:].bitcast(I32), words[0].bitcast(I32))
+            w_scale = keep.tile([P, N], U8, name=f"{name}_scale", align_bytes=64)
+            nc.vector.memset(w_scale[:].bitcast(I32), 0)
+            for q in range(4):
+                queue.dma_start(w_scale[32 * q : 32 * q + 4, :].bitcast(I32), scales[0, 4 * q : 4 * q + 4, :].bitcast(I32))
+            weights.append((w_codes, w_scale))
+
+        lists = [offsets[:, h * LIST_COLS : (h + 1) * LIST_COLS] for h in range(HALVES)]
+        picked = [keep.tile([P, H, PACK], BF16, name=f"picked{h}", align_bytes=64) for h in range(HALVES)]
+        for t in range(PACK):
+            for h in range(HALVES):
+                nc.vector.tensor_copy(picked[h][:, :, t], planes[t][:].indirect(lists[h]))
+
+        gate, cand = [], []
+        for h in range(HALVES):
+            codes = keep.tile([P, H], U32, name=f"codes{h}", align_bytes=64)
+            scale = keep.tile([P, H], U8, name=f"scale{h}", align_bytes=64)
+            nc.vector.quantize_mx(out=codes[:].bitcast(FP8X4), scales=scale[:], in_=picked[h][:].rearrange("p n t -> p (n t)"))
+            acts = []
+            for i, func in enumerate((ACT.Sigmoid, ACT.Tanh)):
+                w_codes, w_scale = weights[i]
+                acc = psum.tile([P, H], F32, name=f"acc{h}{i}")
+                nc.tensor.matmul_mx(out=acc[:], lhsT=w_codes[:].bitcast(FP4X4), lhsT_scale=w_scale[:],
+                                    rhs=codes[:].bitcast(FP8X4), rhs_scale=scale[:], start=True, stop=True)
+                act = keep.tile([P, H], F32, name=f"act{h}{i}")
+                nc.scalar.activation(act[:], acc[:], func)
+                acts.append(act)
+            gate.append(acts[0])
+            cand.append(acts[1])
+
+        passing = keep.tile([P, S], F32, name="passing")
+        nc.vector.tensor_copy(passing[:], res_sb[:].indirect(offsets[:]))
+
+        kept, taken = [], []
+        for h in range(HALVES):
+            a = keep.tile([P, H], F32, name=f"kept{h}")
+            nc.vector.scalar_tensor_tensor(a[:], gate[h][:], 1.0, passing[:, h * H : (h + 1) * H], ALU.subtract, ALU.mult)
+            b = keep.tile([P, H], F32, name=f"taken{h}")
+            nc.vector.tensor_tensor(b[:], gate[h][:], cand[h][:], ALU.mult)
+            kept.append(a)
+            taken.append(b)
+        for h in range(HALVES):
+            result = keep.tile([P, H], F32, name=f"result{h}")
+            nc.vector.tensor_tensor(result[:], taken[h][:], kept[h][:], ALU.subtract)
+            nc.sync.dma_start(out[:, h * H : (h + 1) * H], result[:])

@@ -29,27 +29,28 @@ def tile_picked_highway_tanh_l_kernel(tc, xT, res, w1_words, w1_scales, w2_words
         keep = ctx.enter_context(tc.tile_pool(name="keep", bufs=1))
         psum = ctx.enter_context(tc.psum_pool(name="psum", bufs=1))
 
-        offsets = keep.tile([P, S // 16], U16, name="offsets")
-        nc.sync.dma_start(offsets[:], offs)
+        w_scale = keep.tile([P, 2 * N], U8, name="w_scale", align_bytes=64)
+        scale_words = w_scale[:].bitcast(I32)
+        nc.vector.memset(scale_words, 0)
 
         x_rows = xT.rearrange("(p t) c -> p t c", t=PACK)
-        planes = []
-        for t in range(PACK):
-            plane = keep.tile([P, T], F32, name=f"plane{t}")
-            nc.sync.dma_start(plane[:], x_rows[:, t, :])
-            planes.append(plane)
+        planes = [keep.tile([P, T], F32, name=f"plane{t}") for t in range(PACK)]
+        offsets = keep.tile([P, S // 16], U16, name="offsets")
+        nc.sync.dma_start(planes[0][:], x_rows[:, 0, :])
+        nc.sync.dma_start(offsets[:], offs)
+        for t in range(1, PACK):
+            nc.sync.dma_start(planes[t][:], x_rows[:, t, :])
         res_sb = keep.tile([P, T], F32, name="res_sb")
         nc.sync.dma_start(res_sb[:], res)
 
         weights = []
-        for name, words, scales, queue in (("w2", w2_words, w2_scales, nc.scalar), ("w1", w1_words, w1_scales, nc.gpsimd)):
-            w_codes = keep.tile([P, 2 * N], U8, name=f"{name}_codes", align_bytes=64)
+        for i, (words, scales) in enumerate(((w2_words, w2_scales), (w1_words, w1_scales))):
+            w_codes = keep.tile([P, 2 * N], U8, name=f"w_codes{i}", align_bytes=64)
             nc.scalar.dma_start(w_codes[:].bitcast(I32), words[0].bitcast(I32))
-            w_scale = keep.tile([P, N], U8, name=f"{name}_scale", align_bytes=64)
-            nc.vector.memset(w_scale[:].bitcast(I32), 0)
-            for q in range(4):
-                queue.dma_start(w_scale[32 * q : 32 * q + 4, :].bitcast(I32), scales[0, 4 * q : 4 * q + 4, :].bitcast(I32))
-            weights.append((w_codes, w_scale))
+            nc.scalar.dma_start(w_scale[0:16, i * N : (i + 1) * N].bitcast(I32), scales[0].bitcast(I32))
+            weights.append((w_codes[:], w_scale[:, i * N : (i + 1) * N]))
+        for q in range(1, 4):
+            nc.scalar.dma_start(w_scale[32 * q : 32 * q + 4, :].bitcast(I32), w_scale[4 * q : 4 * q + 4, :].bitcast(I32))
 
         lists = [offsets[:, h * LIST_COLS : (h + 1) * LIST_COLS] for h in range(HALVES)]
         picked = [keep.tile([P, H, PACK], BF16, name=f"picked{h}", align_bytes=64) for h in range(HALVES)]
@@ -64,9 +65,9 @@ def tile_picked_highway_tanh_l_kernel(tc, xT, res, w1_words, w1_scales, w2_words
             nc.vector.quantize_mx(out=codes[:].bitcast(FP8X4), scales=scale[:], in_=picked[h][:].rearrange("p n t -> p (n t)"))
             acts = []
             for i, func in enumerate((ACT.Sigmoid, ACT.Tanh)):
-                w_codes, w_scale = weights[i]
+                wc, ws = weights[i]
                 acc = psum.tile([P, H], F32, name=f"acc{h}{i}")
-                nc.tensor.matmul_mx(out=acc[:], lhsT=w_codes[:].bitcast(FP4X4), lhsT_scale=w_scale[:],
+                nc.tensor.matmul_mx(out=acc[:], lhsT=wc.bitcast(FP4X4), lhsT_scale=ws,
                                     rhs=codes[:].bitcast(FP8X4), rhs_scale=scale[:], start=True, stop=True)
                 act = keep.tile([P, H], F32, name=f"act{h}{i}")
                 nc.scalar.activation(act[:], acc[:], func)
@@ -74,13 +75,14 @@ def tile_picked_highway_tanh_l_kernel(tc, xT, res, w1_words, w1_scales, w2_words
             gate.append(acts[0])
             cand.append(acts[1])
 
-        passing = keep.tile([P, S], F32, name="passing")
-        nc.vector.tensor_copy(passing[:], res_sb[:].indirect(offsets[:]))
+        passing = [keep.tile([P, H], F32, name=f"passing{h}") for h in range(HALVES)]
+        for h in range(HALVES):
+            nc.vector.tensor_copy(passing[h][:], res_sb[:].indirect(lists[h]))
 
         kept, taken = [], []
         for h in range(HALVES):
             a = keep.tile([P, H], F32, name=f"kept{h}")
-            nc.vector.scalar_tensor_tensor(a[:], gate[h][:], 1.0, passing[:, h * H : (h + 1) * H], ALU.subtract, ALU.mult)
+            nc.vector.scalar_tensor_tensor(a[:], gate[h][:], 1.0, passing[h][:], ALU.subtract, ALU.mult)
             b = keep.tile([P, H], F32, name=f"taken{h}")
             nc.vector.tensor_tensor(b[:], gate[h][:], cand[h][:], ALU.mult)
             kept.append(a)

@@ -18,9 +18,14 @@ ALU = mybir.AluOpType
 
 P = 128
 PACK = 4
+QUADRANT = 32
+SCALE_ROWS = 4
+BLOCKS = K // 32
 HALVES = 2
 H = S // HALVES
 LIST_COLS = H // 16
+
+PIECES = ((0, 0, H), (1, 0, H // 2), (1, H // 2, H))
 
 
 def tile_picked_highway_tanh_l_kernel(tc, xT, res, w1_words, w1_scales, w2_words, w2_scales, offs, out):
@@ -30,8 +35,7 @@ def tile_picked_highway_tanh_l_kernel(tc, xT, res, w1_words, w1_scales, w2_words
         psum = ctx.enter_context(tc.psum_pool(name="psum", bufs=1))
 
         w_scale = keep.tile([P, 2 * N], U8, name="w_scale", align_bytes=64)
-        scale_words = w_scale[:].bitcast(I32)
-        nc.vector.memset(scale_words, 0)
+        nc.vector.memset(w_scale[:].bitcast(I32), 0)
 
         x_rows = xT.rearrange("(p t) c -> p t c", t=PACK)
         planes = [keep.tile([P, T], F32, name=f"plane{t}") for t in range(PACK)]
@@ -47,10 +51,13 @@ def tile_picked_highway_tanh_l_kernel(tc, xT, res, w1_words, w1_scales, w2_words
         for i, (words, scales) in enumerate(((w2_words, w2_scales), (w1_words, w1_scales))):
             w_codes = keep.tile([P, 2 * N], U8, name=f"w_codes{i}", align_bytes=64)
             nc.scalar.dma_start(w_codes[:].bitcast(I32), words[0].bitcast(I32))
-            nc.scalar.dma_start(w_scale[0:16, i * N : (i + 1) * N].bitcast(I32), scales[0].bitcast(I32))
+            nc.scalar.dma_start(w_scale[0:BLOCKS, i * N : (i + 1) * N].bitcast(I32), scales[0].bitcast(I32))
             weights.append((w_codes[:], w_scale[:, i * N : (i + 1) * N]))
-        for q in range(1, 4):
-            nc.scalar.dma_start(w_scale[32 * q : 32 * q + 4, :].bitcast(I32), w_scale[4 * q : 4 * q + 4, :].bitcast(I32))
+        for q in range(1, P // QUADRANT):
+            nc.scalar.dma_start(
+                w_scale[QUADRANT * q : QUADRANT * q + SCALE_ROWS, :].bitcast(I32),
+                w_scale[SCALE_ROWS * q : SCALE_ROWS * (q + 1), :].bitcast(I32),
+            )
 
         lists = [offsets[:, h * LIST_COLS : (h + 1) * LIST_COLS] for h in range(HALVES)]
         picked = [keep.tile([P, H, PACK], BF16, name=f"picked{h}", align_bytes=64) for h in range(HALVES)]
@@ -60,34 +67,48 @@ def tile_picked_highway_tanh_l_kernel(tc, xT, res, w1_words, w1_scales, w2_words
 
         gate, cand = [], []
         for h in range(HALVES):
-            codes = keep.tile([P, H], U32, name=f"codes{h}", align_bytes=64)
-            scale = keep.tile([P, H], U8, name=f"scale{h}", align_bytes=64)
-            nc.vector.quantize_mx(out=codes[:].bitcast(FP8X4), scales=scale[:], in_=picked[h][:].rearrange("p n t -> p (n t)"))
-            acts = []
-            for i, func in enumerate((ACT.Sigmoid, ACT.Tanh)):
-                wc, ws = weights[i]
+            x_codes = keep.tile([P, H], U32, name=f"x_codes{h}", align_bytes=64)
+            x_scale = keep.tile([P, H], U8, name=f"x_scale{h}", align_bytes=64)
+            nc.vector.quantize_mx(
+                out=x_codes[:].bitcast(FP8X4), scales=x_scale[:], in_=picked[h][:].rearrange("p n t -> p (n t)")
+            )
+            sums = []
+            for i, (codes, scale) in enumerate(weights):
                 acc = psum.tile([P, H], F32, name=f"acc{h}{i}")
-                nc.tensor.matmul_mx(out=acc[:], lhsT=wc.bitcast(FP4X4), lhsT_scale=ws,
-                                    rhs=codes[:].bitcast(FP8X4), rhs_scale=scale[:], start=True, stop=True)
-                act = keep.tile([P, H], F32, name=f"act{h}{i}")
-                nc.scalar.activation(act[:], acc[:], func)
-                acts.append(act)
-            gate.append(acts[0])
-            cand.append(acts[1])
+                nc.tensor.matmul_mx(
+                    out=acc[:],
+                    lhsT=codes.bitcast(FP4X4),
+                    lhsT_scale=scale,
+                    rhs=x_codes[:].bitcast(FP8X4),
+                    rhs_scale=x_scale[:],
+                    start=True,
+                    stop=True,
+                )
+                sums.append(acc)
+            g = keep.tile([P, H], F32, name=f"gate{h}")
+            nc.scalar.activation(g[:], sums[0][:], ACT.Sigmoid)
+            gate.append(g)
+            for half, lo, hi in PIECES:
+                if half == h:
+                    y = keep.tile([P, hi - lo], F32, name=f"cand{h}_{lo}")
+                    nc.scalar.activation(y[:], sums[1][:, lo:hi], ACT.Tanh)
+                    cand.append(y)
 
         passing = [keep.tile([P, H], F32, name=f"passing{h}") for h in range(HALVES)]
         for h in range(HALVES):
             nc.vector.tensor_copy(passing[h][:], res_sb[:].indirect(lists[h]))
 
-        kept, taken = [], []
+        minus_kept, taken = [], []
         for h in range(HALVES):
-            a = keep.tile([P, H], F32, name=f"kept{h}")
+            a = keep.tile([P, H], F32, name=f"minus_kept{h}")
             nc.vector.scalar_tensor_tensor(a[:], gate[h][:], 1.0, passing[h][:], ALU.subtract, ALU.mult)
-            b = keep.tile([P, H], F32, name=f"taken{h}")
-            nc.vector.tensor_tensor(b[:], gate[h][:], cand[h][:], ALU.mult)
-            kept.append(a)
-            taken.append(b)
-        for h in range(HALVES):
-            result = keep.tile([P, H], F32, name=f"result{h}")
-            nc.vector.tensor_tensor(result[:], taken[h][:], kept[h][:], ALU.subtract)
-            nc.sync.dma_start(out[:, h * H : (h + 1) * H], result[:])
+            minus_kept.append(a)
+            for y, (half, lo, hi) in zip(cand, PIECES):
+                if half == h:
+                    b = keep.tile([P, hi - lo], F32, name=f"taken{h}_{lo}")
+                    nc.vector.tensor_tensor(b[:], gate[h][:, lo:hi], y[:], ALU.mult)
+                    taken.append(b)
+        for b, (h, lo, hi) in zip(taken, PIECES):
+            result = keep.tile([P, hi - lo], F32, name=f"result{h}_{lo}")
+            nc.vector.tensor_tensor(result[:], b[:], minus_kept[h][:, lo:hi], ALU.subtract)
+            nc.sync.dma_start(out[:, h * H + lo : h * H + hi], result[:])

from contextlib import ExitStack

import concourse.mybir as mybir

K, T, S, N = 512, 2048, 512, 128
FLOPS = 2 * 2 * K * N * S

F32 = mybir.dt.float32
BF16 = mybir.dt.bfloat16
I32 = mybir.dt.int32
U32 = mybir.dt.uint32
U16 = mybir.dt.uint16
U8 = mybir.dt.uint8
FP8X4 = mybir.dt.float8_e4m3fn_x4
FP4X4 = mybir.dt.float4_e2m1fn_x4
ACT = mybir.ActivationFunctionType
ALU = mybir.AluOpType

P = 128
PACK = 4
QUADRANT = 32
SCALE_ROWS = 4
BLOCKS = K // 32
HALVES = 2
H = S // HALVES
LIST_COLS = H // 16

PIECES = ((0, 0, H), (1, 0, H // 2), (1, H // 2, H))


def tile_picked_highway_tanh_l_kernel(tc, xT, res, w1_words, w1_scales, w2_words, w2_scales, offs, out):
    nc = tc.nc
    with ExitStack() as ctx:
        keep = ctx.enter_context(tc.tile_pool(name="keep", bufs=1))
        psum = ctx.enter_context(tc.psum_pool(name="psum", bufs=1))

        w_scale = keep.tile([P, 2 * N], U8, name="w_scale", align_bytes=64)
        nc.vector.memset(w_scale[:].bitcast(I32), 0)

        x_rows = xT.rearrange("(p t) c -> p t c", t=PACK)
        planes = [keep.tile([P, T], F32, name=f"plane{t}") for t in range(PACK)]
        offsets = keep.tile([P, S // 16], U16, name="offsets")
        nc.sync.dma_start(planes[0][:], x_rows[:, 0, :])
        nc.sync.dma_start(offsets[:], offs)
        for t in range(1, PACK):
            nc.sync.dma_start(planes[t][:], x_rows[:, t, :])
        res_sb = keep.tile([P, T], F32, name="res_sb")
        nc.sync.dma_start(res_sb[:], res)

        weights = []
        for i, (words, scales) in enumerate(((w2_words, w2_scales), (w1_words, w1_scales))):
            w_codes = keep.tile([P, 2 * N], U8, name=f"w_codes{i}", align_bytes=64)
            nc.scalar.dma_start(w_codes[:].bitcast(I32), words[0].bitcast(I32))
            nc.scalar.dma_start(w_scale[0:BLOCKS, i * N : (i + 1) * N].bitcast(I32), scales[0].bitcast(I32))
            weights.append((w_codes[:], w_scale[:, i * N : (i + 1) * N]))
        for q in range(1, P // QUADRANT):
            nc.scalar.dma_start(
                w_scale[QUADRANT * q : QUADRANT * q + SCALE_ROWS, :].bitcast(I32),
                w_scale[SCALE_ROWS * q : SCALE_ROWS * (q + 1), :].bitcast(I32),
            )

        lists = [offsets[:, h * LIST_COLS : (h + 1) * LIST_COLS] for h in range(HALVES)]
        picked = [keep.tile([P, H, PACK], BF16, name=f"picked{h}", align_bytes=64) for h in range(HALVES)]
        for t in range(PACK):
            for h in range(HALVES):
                nc.vector.tensor_copy(picked[h][:, :, t], planes[t][:].indirect(lists[h]))

        gate, cand = [], []
        for h in range(HALVES):
            x_codes = keep.tile([P, H], U32, name=f"x_codes{h}", align_bytes=64)
            x_scale = keep.tile([P, H], U8, name=f"x_scale{h}", align_bytes=64)
            nc.vector.quantize_mx(
                out=x_codes[:].bitcast(FP8X4), scales=x_scale[:], in_=picked[h][:].rearrange("p n t -> p (n t)")
            )
            sums = []
            for i, (codes, scale) in enumerate(weights):
                acc = psum.tile([P, H], F32, name=f"acc{h}{i}")
                nc.tensor.matmul_mx(
                    out=acc[:],
                    lhsT=codes.bitcast(FP4X4),
                    lhsT_scale=scale,
                    rhs=x_codes[:].bitcast(FP8X4),
                    rhs_scale=x_scale[:],
                    start=True,
                    stop=True,
                )
                sums.append(acc)
            g = keep.tile([P, H], F32, name=f"gate{h}")
            nc.scalar.activation(g[:], sums[0][:], ACT.Sigmoid)
            gate.append(g)
            for half, lo, hi in PIECES:
                if half == h:
                    y = keep.tile([P, hi - lo], F32, name=f"cand{h}_{lo}")
                    nc.scalar.activation(y[:], sums[1][:, lo:hi], ACT.Tanh)
                    cand.append(y)

        passing = [keep.tile([P, H], F32, name=f"passing{h}") for h in range(HALVES)]
        for h in range(HALVES):
            nc.vector.tensor_copy(passing[h][:], res_sb[:].indirect(lists[h]))

        minus_kept, taken = [], []
        for h in range(HALVES):
            a = keep.tile([P, H], F32, name=f"minus_kept{h}")
            nc.vector.scalar_tensor_tensor(a[:], gate[h][:], 1.0, passing[h][:], ALU.subtract, ALU.mult)
            minus_kept.append(a)
            for y, (half, lo, hi) in zip(cand, PIECES):
                if half == h:
                    b = keep.tile([P, hi - lo], F32, name=f"taken{h}_{lo}")
                    nc.vector.tensor_tensor(b[:], gate[h][:, lo:hi], y[:], ALU.mult)
                    taken.append(b)
        for b, (h, lo, hi) in zip(taken, PIECES):
            result = keep.tile([P, hi - lo], F32, name=f"result{h}_{lo}")
            nc.vector.tensor_tensor(result[:], b[:], minus_kept[h][:, lo:hi], ALU.subtract)
            nc.sync.dma_start(out[:, h * H + lo : h * H + hi], result[:])
